import numpy as np
import ml_dtypes


def mxq(x, axis, fmt="e4m3"):
    dtype, down = {"e4m3": (ml_dtypes.float8_e4m3fn, 7), "e5m2": (ml_dtypes.float8_e5m2, 14)}[fmt]
    v = np.moveaxis(np.asarray(x, np.float32).astype(ml_dtypes.bfloat16).astype(np.float64), axis, -1)
    blocks = v.reshape(v.shape[:-1] + (-1, 32))
    amax = np.abs(blocks).max(-1, keepdims=True)
    byte = np.maximum(np.where(amax > 0, np.frexp(amax)[1] - 1 + 127, 0) - down, 1)
    scale = np.exp2(byte - 127.0)
    codes = (blocks / scale).astype(np.float32).astype(dtype).astype(np.float64)
    return np.moveaxis((codes * scale).reshape(v.shape), -1, axis)


WIDE = False


def mx_kscale(k):
    if not WIDE:
        return np.ones(k)
    levels = np.array([10, -10, 5, -5, 0])
    if k % 512:
        return np.exp2(np.random.permutation(np.resize(levels, k // 32))).repeat(32)
    a = np.empty((k // 512, 16))
    for p in range(k // 512):
        a[p, :8] = np.random.permutation(np.resize(levels, 8))
        for g in range(8):
            far = levels[np.abs(levels - a[p, g]) >= 10]
            a[p, g + 8] = far[np.random.randint(len(far))]
    return np.exp2(a.ravel()).repeat(32)


def f64(x):
    return np.asarray(x).astype(np.float64)


def striped(idx):
    return np.tile(np.asarray(idx).reshape(-1, 16).T, (8, 1)).astype(np.uint16)


def unstriped(offs):
    return offs[:16].T.reshape(-1).astype(np.int64)


E2M1 = np.array([0.0, 0.5, 1.0, 1.5, 2.0, 3.0, 4.0, 6.0, -0.0, -0.5, -1.0, -1.5, -2.0, -3.0, -4.0, -6.0])


def pack_weight(w, fmt):
    k, n = w.shape
    w = f64(np.asarray(w, np.float32).astype(ml_dtypes.bfloat16)).reshape(k // 32, 32, n)
    amax = np.abs(w).max(1)
    if fmt == "e4m3":
        byte = np.frexp(amax)[1] - 1 + 127 - 7
    else:
        mant, ex = np.frexp(amax / 6.0)
        byte = np.where(mant > 0.5, ex, ex - 1) + 127
    byte = np.clip(np.where(amax > 0, byte, 1), 1, 254)
    scaled = (w * np.exp2(127.0 - byte)[:, None, :]).reshape(k, n).astype(np.float32)
    by_word = np.ascontiguousarray(scaled.reshape(k // 512, 128, 4, n).transpose(0, 1, 3, 2))
    if fmt == "e4m3":
        words = by_word.astype(ml_dtypes.float8_e4m3fn).view(np.uint8)
    else:
        c = by_word.astype(ml_dtypes.float4_e2m1fn).view(np.uint8) & 0xF
        words = (c[..., 0::2] | (c[..., 1::2] << 4)).reshape(k // 512, 128, 2 * n)
    return np.ascontiguousarray(words), np.ascontiguousarray(byte.astype(np.uint8).reshape(k // 512, 16, n))


def unpack_weight(words, scales, fmt):
    g, _, n = scales.shape
    words = np.ascontiguousarray(words).reshape(g, 128, n, -1)
    if fmt == "e4m3":
        vals = words.view(ml_dtypes.float8_e4m3fn).astype(np.float64)
    else:
        nib = np.empty((g, 128, n, 4), np.uint8)
        nib[..., 0::2] = words & 0xF
        nib[..., 1::2] = words >> 4
        vals = E2M1[nib]
    vals = vals * np.repeat(np.exp2(scales.astype(np.float64) - 127.0), 8, axis=1)[..., None]
    return vals.transpose(0, 1, 3, 2).reshape(g * 512, n)


def sigmoid(v):
    return 1.0 / (1.0 + np.exp(-v))


D, E, T, I, Q = 512, 512, 2048, 512, 128


def setup_inputs():
    n = np.random.standard_normal
    idx = np.random.permutation(T)[:I]
    fd = mx_kscale(D)
    fe = mx_kscale(E)
    keysp = pack_weight(n((D, T)) / fd[:, None], "e4m3")
    valsp = pack_weight(n((E, T)) / fe[:, None], "e4m3")
    return {
        "query": (n((D, Q)) * 0.8 / np.sqrt(D) * fd[:, None]).astype(np.float32),
        "keys_words": keysp[0],
        "keys_scales": keysp[1],
        "th": (np.random.uniform(5.8, 6.1, (Q, 1))).astype(np.float32),
        "steep": (np.random.uniform(1.0, 4.0, (Q, 1))).astype(np.float32),
        "sdot": (np.random.uniform(-0.3, 0.3, (Q, 1))).astype(np.float32),
        "gout": (n((E, Q)) * 1 / np.sqrt(E) * fe[:, None]).astype(np.float32),
        "vals_words": valsp[0],
        "vals_scales": valsp[1],
        "dquery": (n((D, Q)) * 1.0 / np.sqrt(D) * fd[:, None]).astype(np.float32),
        "base": (0.5 * n((Q, T))).astype(np.float32),
        "offs": striped(idx),
    }


def reference(query, keys_words, keys_scales, th, steep, sdot, gout, vals_words, vals_scales, dquery, base, offs):
    idx = unstriped(offs)
    keysu = unpack_weight(keys_words, keys_scales, "e4m3")
    valsu = unpack_weight(vals_words, vals_scales, "e4m3")
    queryq = mxq(f64(query), 0, "e4m3")
    keysidxg = keysu[:, idx]
    a = queryq.T @ keysidxg
    dqueryq = mxq(f64(dquery), 0, "e4m3")
    ta = dqueryq.T @ keysidxg
    b = a - np.max(a, axis=1, keepdims=True)
    p = np.exp(b)
    z = np.sum(p, axis=1, keepdims=True)
    en = np.log(z) - np.sum(p * b, axis=1, keepdims=True) / z
    gt = sigmoid((f64(th) - en) * f64(steep))
    goutq = mxq(f64(gout), 0, "e4m3")
    valsidxg = valsu[:, idx]
    c0 = goutq.T @ valsidxg
    dgt = np.sum(p * c0, axis=1, keepdims=True) / z - f64(sdot)
    den = dgt * gt * (1.0 - gt) * f64(steep) * (-1.0)
    dz = den / z - gt * np.sum(p * c0, axis=1, keepdims=True) / np.square(z) - den * (-1.0) * np.sum(p * b, axis=1, keepdims=True) / np.square(z)
    dp = gt / z * c0 + den * (-1.0) / z * b + dz
    tb = ta
    tp = tb * p
    tz = np.sum(tp, axis=1, keepdims=True)
    ten = tz / z - (np.sum(tp * b + tb * p, axis=1, keepdims=True) - tz * np.sum(p * b, axis=1, keepdims=True) / z) / z
    tgt = ten * (-1.0) * f64(steep) * gt * (1.0 - gt)
    tdgt = (np.sum(tp * c0, axis=1, keepdims=True) - tz * np.sum(p * c0, axis=1, keepdims=True) / z) / z
    tden = ((tdgt * gt + tgt * dgt) * (1.0 - gt) + tgt * (-1.0) * dgt * gt) * f64(steep) * (-1.0)
    tdz = (tden - tz * den / z) / z - (tgt * np.sum(p * c0, axis=1, keepdims=True) + np.sum(tp * c0, axis=1, keepdims=True) * gt - tz * z * 2.0 * gt * np.sum(p * c0, axis=1, keepdims=True) / np.square(z)) / np.square(z) - (tden * (-1.0) * np.sum(p * b, axis=1, keepdims=True) + np.sum(tp * b + tb * p, axis=1, keepdims=True) * den * (-1.0) - tz * z * 2.0 * den * (-1.0) * np.sum(p * b, axis=1, keepdims=True) / np.square(z)) / np.square(z)
    tdp = (tgt - tz * gt / z) / z * c0 + (tden * (-1.0) - tz * den * (-1.0) / z) / z * b + tb * den * (-1.0) / z + tdz
    tdb = (tden * (-1.0) - tz * den * (-1.0) / z) / z * p + tp * den * (-1.0) / z + tdp * p + tp * dp
    gs = tdb * 512.0
    gf = np.zeros((Q, T))
    gf[:, idx] = gs
    y = f64(base) + gf
    return y

@@ -1,0 +1,220 @@
+from contextlib import ExitStack
+
+import concourse.mybir as mybir
+
+F32 = mybir.dt.float32
+BF16 = mybir.dt.bfloat16
+I32 = mybir.dt.int32
+U32 = mybir.dt.uint32
+U16 = mybir.dt.uint16
+U8 = mybir.dt.uint8
+FP8X4 = mybir.dt.float8_e4m3fn_x4
+ALU = mybir.AluOpType
+ACT = mybir.ActivationFunctionType
+AX = mybir.AxisListType
+
+P = 128
+PACK = 4
+TOKENS = 2048
+SLOTS = 512
+ROWS = 128
+OUT_CHUNK = 512
+VALUE_PLANE = 4
+ROOT = 65536.0
+FLOPS = 3 * 2 * 512 * ROWS * SLOTS
+
+
+def tile_attend_hvcertainty_s_kernel(
+    tc, query, keys_words, keys_scales, th, steep, sdot, gout, vals_words, vals_scales, dquery, base, offs, out
+):
+    nc = tc.nc
+    with ExitStack() as ctx:
+        keep = ctx.enter_context(tc.tile_pool(name="keep", bufs=1))
+        reuse = ctx.enter_context(tc.tile_pool(name="reuse", bufs=1))
+        psum = ctx.enter_context(tc.psum_pool(name="psum", bufs=1))
+
+        def sb(name, width, dtype=F32, tag=None):
+            return keep.tile([P, width], dtype, name=name, tag=tag or name, align_bytes=64)
+
+        def words_of(dram):
+            return dram[0].rearrange("p n t -> p (n t)").bitcast(I32)
+
+        def load_scales(queue, tile, dram, first):
+            for r in range(4):
+                queue.dma_start(out=tile[first + r : P : 32, :].bitcast(I32), in_=dram[0, r:16:4, :].bitcast(I32))
+
+        def load_rows(raw, dram):
+            nc.sync.dma_start(out=raw[:], in_=dram.rearrange("(p j) w -> p (j w)", j=PACK))
+            return raw
+
+        def round_rows(name, raw):
+            grouped = sb(name, PACK * ROWS, BF16)
+            nc.scalar.copy(
+                out=grouped[:].rearrange("p (w j) -> p w j", j=PACK),
+                in_=raw[:].rearrange("p (j w) -> p w j", j=PACK),
+            )
+            return grouped
+
+        def quantise(name, grouped, tag):
+            codes = sb(name + "_codes", ROWS, U32, tag=tag)
+            scales = sb(name + "_scales", ROWS, U8)
+            nc.vector.quantize_mx(out=codes[:].bitcast(FP8X4), scales=scales[:], in_=grouped[:])
+            return codes, scales
+
+        def gather(name, window, dtype, tag):
+            picked = sb(name, SLOTS, dtype, tag=tag)
+            nc.vector.tensor_copy(out=picked[:], in_=window[:].indirect(offsets[:]))
+            return picked
+
+        def product(name, rows, words, scales):
+            bank = psum.tile([P, SLOTS], F32, name=name)
+            nc.tensor.matmul_mx(
+                out=bank[:], lhsT=rows[0][:].bitcast(FP8X4), lhsT_scale=rows[1][:],
+                rhs=words[:].bitcast(FP8X4), rhs_scale=scales, start=True, stop=True,
+            )
+            return bank
+
+        def fma(name, x, scale, bias, dst=None, width=1):
+            res = dst if dst is not None else sb(name, width)[:]
+            func = ACT.Copy if isinstance(bias, float) else ACT.Identity
+            nc.scalar.activation(out=res, in_=x, func=func, scale=scale, bias=bias)
+            return res
+
+        def weighted(name, x, shift, op, weights, total):
+            res = sb(name, SLOTS)
+            nc.vector.scalar_tensor_tensor(
+                out=res[:], in0=x, scalar=shift, in1=weights, op0=op, op1=ALU.mult, accum_out=total
+            )
+            return res
+
+        offsets = keep.tile([P, SLOTS // 16], U16, name="offsets")
+        key_scales = reuse.tile([P, TOKENS], U8, name="key_scales", offset=4 * TOKENS - TOKENS // 2)
+        val_scales = sb("val_scales", TOKENS, U8)
+        placed = sb("placed", TOKENS)
+        nc.vector.memset(key_scales[:].bitcast(I32), 0)
+        nc.vector.memset(val_scales[:].bitcast(I32), 0)
+        nc.vector.memset(placed[:], 0.0)
+
+        nc.sync.dma_start(offsets[:], offs)
+        load_scales(nc.scalar, key_scales, keys_scales, 0)
+        key_words = sb("key_words", TOKENS, U32)
+        nc.sync.dma_start(out=key_words[:].bitcast(I32), in_=words_of(keys_words))
+        query_raw = load_rows(sb("query_raw", PACK * ROWS, tag="slot_b"), query)
+        dquery_raw = load_rows(sb("dquery_raw", PACK * ROWS, tag="slot_c"), dquery)
+        load_scales(nc.gpsimd, val_scales, vals_scales, VALUE_PLANE)
+        consts = sb("consts", 3)
+        for i, value in enumerate((1.0 / ROOT, ROOT, -2.0)):
+            nc.vector.memset(consts[:, i : i + 1], value)
+
+        key_scales_g = gather("key_scales_g", key_scales, U8, "scales_g")
+        gout_raw = load_rows(reuse.tile([P, PACK * ROWS], F32, name="gout_raw", offset=4 * TOKENS), gout)
+        val_words = reuse.tile([P, TOKENS], U32, name="val_words", offset=0)
+        nc.sync.dma_start(out=val_words[:].bitcast(I32), in_=words_of(vals_words))
+        query_bf = round_rows("query_bf", query_raw)
+        row_cols = sb("row_cols", 24, tag="slot_b")
+        steep_col, th_col, sdot_col = row_cols[:, 0:1], row_cols[:, 8:9], row_cols[:, 16:17]
+        nc.scalar.dma_start(out=steep_col, in_=steep)
+        nc.scalar.dma_start(out=th_col, in_=th)
+        nc.scalar.dma_start(out=sdot_col, in_=sdot)
+        dquery_bf = round_rows("dquery_bf", dquery_raw)
+        base_sb = sb("base_sb", TOKENS, tag="slot_c")
+        nc.sync.dma_start(out=base_sb[:], in_=base)
+
+        key_words_g = gather("key_words_g", key_words, U32, "words_g")
+        query_mx = quantise("query", query_bf, "codes_a")
+        a = product("a", query_mx, key_words_g, key_scales_g[:])
+        dquery_mx = quantise("dquery", dquery_bf, "codes_b")
+        t = product("t", dquery_mx, key_words_g, key_scales_g[:])
+        gout_bf = round_rows("gout_bf", gout_raw)
+
+        neg_max = sb("neg_max", 1)
+        nc.vector.tensor_reduce(out=neg_max[:], in_=a[:], axis=AX.X, op=ALU.max, negate=True)
+        p = sb("p", SLOTS)
+        z = sb("z", 1)
+        nc.scalar.activation(out=p[:], in_=a[:], func=ACT.Exp, bias=neg_max[:], scale=1.0, accum_out=z[:])
+        root = sb("root", 1)
+        nc.gpsimd.tensor_tensor(out=root[:], in0=z[:], in1=consts[:, 0:1], op=ALU.pow)
+        val_scales_g = gather("val_scales_g", val_scales, U8, "scales_g")
+        gout_mx = quantise("gout", gout_bf, "codes_b")
+        inv_z = sb("inv_z", 1)
+        nc.vector.reciprocal(out=inv_z[:], in_=z[:])
+
+        sums = sb("sums", 5)
+        weighted("scrap_b", a[:], neg_max[:], ALU.add, p[:], sums[:, 0:1])
+        pt = weighted("pt", t[:], 1.0, ALU.mult, p[:], sums[:, 1:2])
+        b = fma("b", a[:], 1.0, neg_max[:], width=SLOTS)
+        val_words_g = gather("val_words_g", val_words, U32, "words_g")
+        c = product("c", gout_mx, val_words_g, val_scales_g[VALUE_PLANE:P, :])
+        weighted("scrap_tb", a[:], neg_max[:], ALU.add, pt[:], sums[:, 2:3])
+        weighted("scrap_c", c[:], 1.0, ALU.mult, p[:], sums[:, 3:4])
+        weighted("scrap_tc", c[:], 1.0, ALU.mult, pt[:], sums[:, 4:5])
+
+        back = sb("back", 1)
+        nc.scalar.activation(out=back[:], in_=root[:], func=ACT.Exp, scale=-ROOT, bias=consts[:, 1:2])
+        guess = fma("guess", root[:], ROOT, -ROOT)
+        half_s = fma("half_s", steep_col, 0.5, 0.0)
+        neg_half_s = fma("neg_half_s", steep_col, -0.5, 0.0)
+        quarter_s = fma("quarter_s", steep_col, 0.25, 0.0)
+        th_less = fma("th_less", th_col, 1.0, -0.5)
+        by_nsh = sb("by_nsh", 3)
+        fma("", sdot_col, 1.0, 0.0, dst=by_nsh[:, 1:2])
+        neg_inv_z = fma("", inv_z[:], -1.0, 0.0, dst=by_nsh[:, 0:1])
+        square = sb("square", 1)
+        nc.scalar.activation(out=square[:], in_=back[:], func=ACT.Square, scale=z[:], bias=consts[:, 2:3])
+        inv_z_256 = fma("inv_z_256", inv_z[:], 256.0, 0.0)
+        th_guess = fma("th_guess", guess, -1.0, th_less)
+        gate_shift = fma("gate_shift", th_guess, half_s, 0.0)
+        neg_b = fma("neg_b", sums[:, 0:1], neg_inv_z, 0.0)
+        gate_bias = fma("gate_bias", neg_b, neg_half_s, gate_shift)
+        neg_t = fma("neg_t", sums[:, 1:2], neg_inv_z, 0.0)
+        tau = sb("tau", 1)
+        nc.scalar.activation(out=tau[:], in_=square[:], func=ACT.Tanh, scale=quarter_s, bias=gate_bias)
+        mean_tb = fma("mean_tb", neg_t, neg_b, 0.0)
+        one_minus_b = fma("one_minus_b", neg_b, 1.0, 1.0)
+        t_over_z = fma("t_over_z", neg_t, neg_inv_z, 0.0)
+        neg_sh = fma("neg_sh", tau[:], half_s, neg_half_s)
+        kappa = fma("", tau[:], inv_z_256, inv_z_256, dst=by_nsh[:, 2:3])
+        by_k2 = sb("by_k2", 2)
+        sg = fma("", tau[:], half_s, half_s, dst=by_k2[:, 0:1])
+        times_nsh = fma("times_nsh", by_nsh[:], neg_sh, 0.0, width=3)
+        one_plus_sh = fma("one_plus_sh", neg_sh, -1.0, 1.0)
+        fma("", sg, neg_b, one_plus_sh, dst=by_k2[:, 1:2])
+        k7 = fma("k7", times_nsh[:, 2:3], neg_b, kappa)
+        neg_cov = fma("neg_cov", sums[:, 2:3], neg_inv_z, mean_tb)
+        shift = fma("shift", neg_cov, neg_sh, neg_t)
+        k2 = fma("k2", neg_cov, kappa, 0.0)
+        halves = [slice(0, SLOTS // 2), slice(SLOTS // 2, SLOTS)]
+        lam = fma("lam", sums[:, 3:4], times_nsh[:, 0:1], times_nsh[:, 1:2])
+        mean_tc = fma("mean_tc", sums[:, 3:4], t_over_z, 0.0)
+        neg_c = fma("neg_c", sums[:, 3:4], neg_inv_z, 0.0)
+        times_k2 = fma("times_k2", by_k2[:], k2, 0.0, width=2)
+        neg_cov_tc = fma("neg_cov_tc", sums[:, 4:5], neg_inv_z, mean_tc)
+        mu = fma("mu", lam, one_minus_b, neg_c)
+        times_lam = fma("times_lam", times_k2, lam, 0.0, width=2)
+        beta = fma("beta", neg_cov_tc, times_nsh[:, 2:3], times_lam[:, 0:1])
+        gamma = fma("gamma", neg_cov_tc, k7, times_lam[:, 1:2])
+        te = sb("te", SLOTS)
+        for h in halves:
+            fma("", t[:, h], 1.0, shift, dst=te[:, h])
+
+        linear = sb("linear", SLOTS)
+        inner = sb("inner", SLOTS)
+        cross = sb("cross", SLOTS)
+        bracket = sb("bracket", SLOTS)
+        for h in halves:
+            fma("", b[:, h], beta, gamma, dst=linear[:, h])
+        for h in halves:
+            nc.vector.scalar_tensor_tensor(out=inner[:, h], in0=b[:, h], scalar=lam, in1=c[:, h], op0=ALU.mult, op1=ALU.add)
+        for h in halves:
+            nc.vector.scalar_tensor_tensor(out=cross[:, h], in0=inner[:, h], scalar=mu, in1=te[:, h], op0=ALU.add, op1=ALU.mult)
+        for h in halves:
+            nc.vector.scalar_tensor_tensor(
+                out=bracket[:, h], in0=cross[:, h], scalar=kappa, in1=linear[:, h], op0=ALU.mult, op1=ALU.add
+            )
+        nc.vector.tensor_tensor(out=placed[:].indirect(offsets[:]), in0=p[:], in1=bracket[:], op=ALU.mult)
+
+        for i, c0 in enumerate(range(0, TOKENS, OUT_CHUNK)):
+            cols = slice(c0, c0 + OUT_CHUNK)
+            result = sb("result_%d" % i, OUT_CHUNK)
+            nc.vector.tensor_tensor(out=result[:], in0=base_sb[:, cols], in1=placed[:, cols], op=ALU.add)
+            (nc.sync, nc.scalar)[i % 2].dma_start(out=out[:, cols], in_=result[:])

@@ -18,7 +18,7 @@ PACK = 4
 TOKENS = 2048
 SLOTS = 512
 ROWS = 128
-OUT_CHUNK = 512
+OUT_WIDTHS = (256, 512, 512, 512, 256)
 VALUE_PLANE = 4
 ROOT = 65536.0
 FLOPS = 3 * 2 * 512 * ROWS * SLOTS
@@ -74,14 +74,14 @@ def tile_attend_hvcertainty_s_kernel(
             )
             return bank
 
-        def fma(name, x, scale, bias, dst=None, width=1):
-            res = dst if dst is not None else sb(name, width)[:]
+        def fma(name, x, scale, bias, dst=None, width=1, tag=None):
+            res = dst if dst is not None else sb(name, width, tag=tag)[:]
             func = ACT.Copy if isinstance(bias, float) else ACT.Identity
             nc.scalar.activation(out=res, in_=x, func=func, scale=scale, bias=bias)
             return res
 
-        def weighted(name, x, shift, op, weights, total):
-            res = sb(name, SLOTS)
+        def weighted(name, x, shift, op, weights, total, tag=None):
+            res = sb(name, SLOTS, tag=tag)
             nc.vector.scalar_tensor_tensor(
                 out=res[:], in0=x, scalar=shift, in1=weights, op0=op, op1=ALU.mult, accum_out=total
             )
@@ -93,13 +93,14 @@ def tile_attend_hvcertainty_s_kernel(
         placed = sb("placed", TOKENS)
         nc.vector.memset(key_scales[:].bitcast(I32), 0)
         nc.vector.memset(val_scales[:].bitcast(I32), 0)
-        nc.vector.memset(placed[:], 0.0)
+        nc.vector.memset(placed[:, : TOKENS // 2 + 1], 0.0)
+        nc.vector.memset(placed[:, TOKENS // 2 + 1 :], 0.0)
 
         nc.sync.dma_start(offsets[:], offs)
         load_scales(nc.scalar, key_scales, keys_scales, 0)
+        query_raw = load_rows(sb("query_raw", PACK * ROWS, tag="slot_b"), query)
         key_words = sb("key_words", TOKENS, U32)
         nc.sync.dma_start(out=key_words[:].bitcast(I32), in_=words_of(keys_words))
-        query_raw = load_rows(sb("query_raw", PACK * ROWS, tag="slot_b"), query)
         dquery_raw = load_rows(sb("dquery_raw", PACK * ROWS, tag="slot_c"), dquery)
         load_scales(nc.gpsimd, val_scales, vals_scales, VALUE_PLANE)
         consts = sb("consts", 3)
@@ -120,10 +121,10 @@ def tile_attend_hvcertainty_s_kernel(
         base_sb = sb("base_sb", TOKENS, tag="slot_c")
         nc.sync.dma_start(out=base_sb[:], in_=base)
 
-        key_words_g = gather("key_words_g", key_words, U32, "words_g")
         query_mx = quantise("query", query_bf, "codes_a")
+        key_words_g = gather("key_words_g", key_words, U32, "words_g")
         a = product("a", query_mx, key_words_g, key_scales_g[:])
-        dquery_mx = quantise("dquery", dquery_bf, "codes_b")
+        dquery_mx = quantise("dquery", dquery_bf, "key_words")
         t = product("t", dquery_mx, key_words_g, key_scales_g[:])
         gout_bf = round_rows("gout_bf", gout_raw)
 
@@ -135,64 +136,61 @@ def tile_attend_hvcertainty_s_kernel(
         root = sb("root", 1)
         nc.gpsimd.tensor_tensor(out=root[:], in0=z[:], in1=consts[:, 0:1], op=ALU.pow)
         val_scales_g = gather("val_scales_g", val_scales, U8, "scales_g")
-        gout_mx = quantise("gout", gout_bf, "codes_b")
-        inv_z = sb("inv_z", 1)
-        nc.vector.reciprocal(out=inv_z[:], in_=z[:])
+        gout_mx = quantise("gout", gout_bf, "words_g")
+        by_sh = sb("by_sh", 2)
+        inv_z = by_sh[:, 0:1]
+        nc.vector.reciprocal(out=inv_z, in_=z[:])
 
         sums = sb("sums", 5)
-        weighted("scrap_b", a[:], neg_max[:], ALU.add, p[:], sums[:, 0:1])
+        weighted("scrap_b", a[:], neg_max[:], ALU.add, p[:], sums[:, 0:1], "scrap_b")
         pt = weighted("pt", t[:], 1.0, ALU.mult, p[:], sums[:, 1:2])
-        b = fma("b", a[:], 1.0, neg_max[:], width=SLOTS)
-        val_words_g = gather("val_words_g", val_words, U32, "words_g")
+        val_words_g = gather("val_words_g", val_words, U32, "scrap_b")
         c = product("c", gout_mx, val_words_g, val_scales_g[VALUE_PLANE:P, :])
-        weighted("scrap_tb", a[:], neg_max[:], ALU.add, pt[:], sums[:, 2:3])
-        weighted("scrap_c", c[:], 1.0, ALU.mult, p[:], sums[:, 3:4])
-        weighted("scrap_tc", c[:], 1.0, ALU.mult, pt[:], sums[:, 4:5])
 
-        back = sb("back", 1)
-        nc.scalar.activation(out=back[:], in_=root[:], func=ACT.Exp, scale=-ROOT, bias=consts[:, 1:2])
-        guess = fma("guess", root[:], ROOT, -ROOT)
         half_s = fma("half_s", steep_col, 0.5, 0.0)
         neg_half_s = fma("neg_half_s", steep_col, -0.5, 0.0)
         quarter_s = fma("quarter_s", steep_col, 0.25, 0.0)
-        th_less = fma("th_less", th_col, 1.0, -0.5)
-        by_nsh = sb("by_nsh", 3)
-        fma("", sdot_col, 1.0, 0.0, dst=by_nsh[:, 1:2])
-        neg_inv_z = fma("", inv_z[:], -1.0, 0.0, dst=by_nsh[:, 0:1])
-        square = sb("square", 1)
+        below_half_s = fma("below_half_s", steep_col, -0.5, -1.0)
+        th_half_s = fma("th_half_s", th_col, half_s, quarter_s)
+        fma("", sdot_col, -1.0, 0.0, dst=by_sh[:, 1:2])
+        neg_inv_z = fma("neg_inv_z", inv_z, -1.0, 0.0)
+        inv_z_256 = fma("inv_z_256", inv_z, 256.0, 0.0)
+        back = sb("back", 1)
+        nc.scalar.activation(out=back[:], in_=root[:], func=ACT.Exp, scale=-ROOT, bias=consts[:, 1:2])
+        guess = fma("guess", root[:], ROOT, -ROOT)
+        one_minus_b = fma("one_minus_b", sums[:, 0:1], neg_inv_z, 1.0)
+        square = sb("square", 1, tag="square")
         nc.scalar.activation(out=square[:], in_=back[:], func=ACT.Square, scale=z[:], bias=consts[:, 2:3])
-        inv_z_256 = fma("inv_z_256", inv_z[:], 256.0, 0.0)
-        th_guess = fma("th_guess", guess, -1.0, th_less)
-        gate_shift = fma("gate_shift", th_guess, half_s, 0.0)
-        neg_b = fma("neg_b", sums[:, 0:1], neg_inv_z, 0.0)
-        gate_bias = fma("gate_bias", neg_b, neg_half_s, gate_shift)
+        gate_shift = fma("gate_shift", guess, neg_half_s, th_half_s)
+        centre = fma("centre", neg_max[:], 1.0, one_minus_b)
+        gate_bias = fma("gate_bias", one_minus_b, neg_half_s, gate_shift)
         neg_t = fma("neg_t", sums[:, 1:2], neg_inv_z, 0.0)
         tau = sb("tau", 1)
         nc.scalar.activation(out=tau[:], in_=square[:], func=ACT.Tanh, scale=quarter_s, bias=gate_bias)
-        mean_tb = fma("mean_tb", neg_t, neg_b, 0.0)
-        one_minus_b = fma("one_minus_b", neg_b, 1.0, 1.0)
-        t_over_z = fma("t_over_z", neg_t, neg_inv_z, 0.0)
-        neg_sh = fma("neg_sh", tau[:], half_s, neg_half_s)
-        kappa = fma("", tau[:], inv_z_256, inv_z_256, dst=by_nsh[:, 2:3])
-        by_k2 = sb("by_k2", 2)
-        sg = fma("", tau[:], half_s, half_s, dst=by_k2[:, 0:1])
-        times_nsh = fma("times_nsh", by_nsh[:], neg_sh, 0.0, width=3)
-        one_plus_sh = fma("one_plus_sh", neg_sh, -1.0, 1.0)
-        fma("", sg, neg_b, one_plus_sh, dst=by_k2[:, 1:2])
-        k7 = fma("k7", times_nsh[:, 2:3], neg_b, kappa)
-        neg_cov = fma("neg_cov", sums[:, 2:3], neg_inv_z, mean_tb)
-        shift = fma("shift", neg_cov, neg_sh, neg_t)
-        k2 = fma("k2", neg_cov, kappa, 0.0)
+        b = fma("b", a[:], 1.0, centre, width=SLOTS, tag="square")
+        weighted("scrap_tb", b, 1.0, ALU.mult, pt[:], sums[:, 2:3])
+        weighted("scrap_c", c[:], 1.0, ALU.mult, p[:], sums[:, 3:4])
+        weighted("scrap_tc", c[:], 1.0, ALU.mult, pt[:], sums[:, 4:5])
+        neg_t_over_z = fma("neg_t_over_z", neg_t, inv_z, 0.0)
+        by_kappa = sb("by_kappa", 4)
+        sh = fma("", tau[:], neg_half_s, half_s, dst=by_kappa[:, 0:1])
+        kappa = fma("kappa", tau[:], inv_z_256, inv_z_256)
+        fma("", tau[:], half_s, below_half_s, dst=by_kappa[:, 1:2])
+        fma("", tau[:], neg_half_s, neg_half_s, dst=by_kappa[:, 2:3])
+        fma("", tau[:], steep_col, -1.0, dst=by_kappa[:, 3:4])
+        times_sh = fma("times_sh", by_sh[:], sh, 0.0, width=2)
+        times_kappa = fma("times_kappa", by_kappa[:], kappa, 0.0, width=4)
+        cov_tb = fma("cov_tb", sums[:, 2:3], inv_z, neg_t)
+        shift = fma("shift", cov_tb, sh, neg_t)
+        times_cov = fma("times_cov", times_kappa[:, 2:4], cov_tb, 0.0, width=2)
         halves = [slice(0, SLOTS // 2), slice(SLOTS // 2, SLOTS)]
-        lam = fma("lam", sums[:, 3:4], times_nsh[:, 0:1], times_nsh[:, 1:2])
-        mean_tc = fma("mean_tc", sums[:, 3:4], t_over_z, 0.0)
+        lam = fma("lam", sums[:, 3:4], times_sh[:, 0:1], times_sh[:, 1:2])
+        neg_tc = fma("neg_tc", sums[:, 3:4], neg_t_over_z, 0.0)
         neg_c = fma("neg_c", sums[:, 3:4], neg_inv_z, 0.0)
-        times_k2 = fma("times_k2", by_k2[:], k2, 0.0, width=2)
-        neg_cov_tc = fma("neg_cov_tc", sums[:, 4:5], neg_inv_z, mean_tc)
-        mu = fma("mu", lam, one_minus_b, neg_c)
-        times_lam = fma("times_lam", times_k2, lam, 0.0, width=2)
-        beta = fma("beta", neg_cov_tc, times_nsh[:, 2:3], times_lam[:, 0:1])
-        gamma = fma("gamma", neg_cov_tc, k7, times_lam[:, 1:2])
+        times_lam = fma("times_lam", times_cov, lam, 0.0, width=2)
+        cov_tc = fma("cov_tc", sums[:, 4:5], inv_z, neg_tc)
+        beta = fma("beta", cov_tc, times_kappa[:, 0:1], times_lam[:, 0:1])
+        gamma = fma("gamma", cov_tc, times_kappa[:, 1:2], times_lam[:, 1:2])
         te = sb("te", SLOTS)
         for h in halves:
             fma("", t[:, h], 1.0, shift, dst=te[:, h])
@@ -206,15 +204,16 @@ def tile_attend_hvcertainty_s_kernel(
         for h in halves:
             nc.vector.scalar_tensor_tensor(out=inner[:, h], in0=b[:, h], scalar=lam, in1=c[:, h], op0=ALU.mult, op1=ALU.add)
         for h in halves:
-            nc.vector.scalar_tensor_tensor(out=cross[:, h], in0=inner[:, h], scalar=mu, in1=te[:, h], op0=ALU.add, op1=ALU.mult)
+            nc.vector.scalar_tensor_tensor(out=cross[:, h], in0=inner[:, h], scalar=neg_c, in1=te[:, h], op0=ALU.add, op1=ALU.mult)
         for h in halves:
             nc.vector.scalar_tensor_tensor(
                 out=bracket[:, h], in0=cross[:, h], scalar=kappa, in1=linear[:, h], op0=ALU.mult, op1=ALU.add
             )
         nc.vector.tensor_tensor(out=placed[:].indirect(offsets[:]), in0=p[:], in1=bracket[:], op=ALU.mult)
 
-        for i, c0 in enumerate(range(0, TOKENS, OUT_CHUNK)):
-            cols = slice(c0, c0 + OUT_CHUNK)
-            result = sb("result_%d" % i, OUT_CHUNK)
+        for i, width in enumerate(OUT_WIDTHS):
+            c0 = sum(OUT_WIDTHS[:i])
+            cols = slice(c0, c0 + width)
+            result = sb("result_%d" % i, width)
             nc.vector.tensor_tensor(out=result[:], in0=base_sb[:, cols], in1=placed[:, cols], op=ALU.add)
             (nc.sync, nc.scalar)[i % 2].dma_start(out=out[:, cols], in_=result[:])

@@ -30,7 +30,6 @@ def tile_attend_hvcertainty_s_kernel(
     nc = tc.nc
     with ExitStack() as ctx:
         keep = ctx.enter_context(tc.tile_pool(name="keep", bufs=1))
-        reuse = ctx.enter_context(tc.tile_pool(name="reuse", bufs=1))
         psum = ctx.enter_context(tc.psum_pool(name="psum", bufs=1))
 
         def sb(name, width, dtype=F32, tag=None):
@@ -88,45 +87,48 @@ def tile_attend_hvcertainty_s_kernel(
             return res
 
         offsets = keep.tile([P, SLOTS // 16], U16, name="offsets")
-        key_scales = reuse.tile([P, TOKENS], U8, name="key_scales", offset=4 * TOKENS - TOKENS // 2)
+        key_scales = sb("key_scales", TOKENS, U8)
         val_scales = sb("val_scales", TOKENS, U8)
         placed = sb("placed", TOKENS)
-        nc.vector.memset(key_scales[:].bitcast(I32), 0)
-        nc.vector.memset(val_scales[:].bitcast(I32), 0)
+        ones = sb("ones", 1, tag="key_words")
+        consts = sb("consts", 3)
+        nc.vector.memset(ones[:], 1.0)
+        nc.vector.memset(key_scales[:, : TOKENS // 2].bitcast(I32), 0)
+        nc.gpsimd.memset(key_scales[:, TOKENS // 2 :].bitcast(I32), 0)
+        nc.gpsimd.memset(val_scales[:].bitcast(I32), 0)
+        nc.vector.tensor_scalar_mul(consts[:, 0:1], ones[:], 1.0 / ROOT)
+        nc.vector.memset(consts[:, 1:2], ROOT)
+        nc.vector.memset(consts[:, 2:3], -2.0)
         nc.vector.memset(placed[:, : TOKENS // 2 + 1], 0.0)
         nc.vector.memset(placed[:, TOKENS // 2 + 1 :], 0.0)
 
         nc.sync.dma_start(offsets[:], offs)
-        load_scales(nc.scalar, key_scales, keys_scales, 0)
-        query_raw = load_rows(sb("query_raw", PACK * ROWS, tag="slot_b"), query)
+        query_raw = load_rows(sb("query_raw", PACK * ROWS), query)
+        dquery_raw = load_rows(sb("dquery_raw", PACK * ROWS), dquery)
+        load_scales(nc.sync, key_scales, keys_scales, 0)
         key_words = sb("key_words", TOKENS, U32)
         nc.sync.dma_start(out=key_words[:].bitcast(I32), in_=words_of(keys_words))
-        dquery_raw = load_rows(sb("dquery_raw", PACK * ROWS, tag="slot_c"), dquery)
         load_scales(nc.gpsimd, val_scales, vals_scales, VALUE_PLANE)
-        consts = sb("consts", 3)
-        for i, value in enumerate((1.0 / ROOT, ROOT, -2.0)):
-            nc.vector.memset(consts[:, i : i + 1], value)
 
         key_scales_g = gather("key_scales_g", key_scales, U8, "scales_g")
-        gout_raw = load_rows(reuse.tile([P, PACK * ROWS], F32, name="gout_raw", offset=4 * TOKENS), gout)
-        val_words = reuse.tile([P, TOKENS], U32, name="val_words", offset=0)
-        nc.sync.dma_start(out=val_words[:].bitcast(I32), in_=words_of(vals_words))
         query_bf = round_rows("query_bf", query_raw)
-        row_cols = sb("row_cols", 24, tag="slot_b")
+        gout_raw = load_rows(sb("gout_raw", PACK * ROWS, tag="query_raw"), gout)
+        query_mx = quantise("query", query_bf, None)
+        row_cols = sb("row_cols", 24, tag="query_bf")
         steep_col, th_col, sdot_col = row_cols[:, 0:1], row_cols[:, 8:9], row_cols[:, 16:17]
-        nc.scalar.dma_start(out=steep_col, in_=steep)
-        nc.scalar.dma_start(out=th_col, in_=th)
-        nc.scalar.dma_start(out=sdot_col, in_=sdot)
-        dquery_bf = round_rows("dquery_bf", dquery_raw)
-        base_sb = sb("base_sb", TOKENS, tag="slot_c")
-        nc.sync.dma_start(out=base_sb[:], in_=base)
+        nc.sync.dma_start(out=steep_col, in_=steep)
+        nc.sync.dma_start(out=th_col, in_=th)
+        nc.sync.dma_start(out=sdot_col, in_=sdot)
+        val_words = sb("val_words", TOKENS, U32, tag="key_scales")
+        nc.sync.dma_start(out=val_words[:].bitcast(I32), in_=words_of(vals_words))
+        dquery_mx = quantise("dquery", round_rows("dquery_bf", dquery_raw), None)
 
-        query_mx = quantise("query", query_bf, "codes_a")
         key_words_g = gather("key_words_g", key_words, U32, "words_g")
         a = product("a", query_mx, key_words_g, key_scales_g[:])
-        dquery_mx = quantise("dquery", dquery_bf, "key_words")
         t = product("t", dquery_mx, key_words_g, key_scales_g[:])
-        gout_bf = round_rows("gout_bf", gout_raw)
+        gout_mx = quantise("gout", round_rows("gout_bf", gout_raw), "key_words")
+        base_sb = sb("base_sb", TOKENS, tag="words_g")
+        nc.sync.dma_start(out=base_sb[:], in_=base)
 
         neg_max = sb("neg_max", 1)
         nc.vector.tensor_reduce(out=neg_max[:], in_=a[:], axis=AX.X, op=ALU.max, negate=True)
@@ -136,7 +138,6 @@ def tile_attend_hvcertainty_s_kernel(
         root = sb("root", 1)
         nc.gpsimd.tensor_tensor(out=root[:], in0=z[:], in1=consts[:, 0:1], op=ALU.pow)
         val_scales_g = gather("val_scales_g", val_scales, U8, "scales_g")
-        gout_mx = quantise("gout", gout_bf, "words_g")
         by_sh = sb("by_sh", 2)
         inv_z = by_sh[:, 0:1]
         nc.vector.reciprocal(out=inv_z, in_=z[:])
@@ -168,7 +169,7 @@ def tile_attend_hvcertainty_s_kernel(
         tau = sb("tau", 1)
         nc.scalar.activation(out=tau[:], in_=square[:], func=ACT.Tanh, scale=quarter_s, bias=gate_bias)
         b = fma("b", a[:], 1.0, centre, width=SLOTS, tag="square")
-        weighted("scrap_tb", b, 1.0, ALU.mult, pt[:], sums[:, 2:3])
+        weighted("scrap_tb", b, 1.0, ALU.mult, pt[:], sums[:, 2:3], "key_scales")
         weighted("scrap_c", c[:], 1.0, ALU.mult, p[:], sums[:, 3:4])
         weighted("scrap_tc", c[:], 1.0, ALU.mult, pt[:], sums[:, 4:5])
         neg_t_over_z = fma("neg_t_over_z", neg_t, inv_z, 0.0)

from contextlib import ExitStack

import concourse.mybir as mybir

F32 = mybir.dt.float32
BF16 = mybir.dt.bfloat16
I32 = mybir.dt.int32
U32 = mybir.dt.uint32
U16 = mybir.dt.uint16
U8 = mybir.dt.uint8
FP8X4 = mybir.dt.float8_e4m3fn_x4
ALU = mybir.AluOpType
ACT = mybir.ActivationFunctionType
AX = mybir.AxisListType

P = 128
PACK = 4
TOKENS = 2048
SLOTS = 512
ROWS = 128
OUT_WIDTHS = (256, 512, 512, 512, 256)
VALUE_PLANE = 4
ROOT = 65536.0
FLOPS = 3 * 2 * 512 * ROWS * SLOTS


def tile_attend_hvcertainty_s_kernel(
    tc, query, keys_words, keys_scales, th, steep, sdot, gout, vals_words, vals_scales, dquery, base, offs, out
):
    nc = tc.nc
    with ExitStack() as ctx:
        keep = ctx.enter_context(tc.tile_pool(name="keep", bufs=1))
        psum = ctx.enter_context(tc.psum_pool(name="psum", bufs=1))

        def sb(name, width, dtype=F32, tag=None):
            return keep.tile([P, width], dtype, name=name, tag=tag or name, align_bytes=64)

        def words_of(dram):
            return dram[0].rearrange("p n t -> p (n t)").bitcast(I32)

        def load_scales(queue, tile, dram, first):
            for r in range(4):
                queue.dma_start(out=tile[first + r : P : 32, :].bitcast(I32), in_=dram[0, r:16:4, :].bitcast(I32))

        def load_rows(raw, dram):
            nc.sync.dma_start(out=raw[:], in_=dram.rearrange("(p j) w -> p (j w)", j=PACK))
            return raw

        def round_rows(name, raw):
            grouped = sb(name, PACK * ROWS, BF16)
            nc.scalar.copy(
                out=grouped[:].rearrange("p (w j) -> p w j", j=PACK),
                in_=raw[:].rearrange("p (j w) -> p w j", j=PACK),
            )
            return grouped

        def quantise(name, grouped, tag):
            codes = sb(name + "_codes", ROWS, U32, tag=tag)
            scales = sb(name + "_scales", ROWS, U8)
            nc.vector.quantize_mx(out=codes[:].bitcast(FP8X4), scales=scales[:], in_=grouped[:])
            return codes, scales

        def gather(name, window, dtype, tag):
            picked = sb(name, SLOTS, dtype, tag=tag)
            nc.vector.tensor_copy(out=picked[:], in_=window[:].indirect(offsets[:]))
            return picked

        def product(name, rows, words, scales):
            bank = psum.tile([P, SLOTS], F32, name=name)
            nc.tensor.matmul_mx(
                out=bank[:], lhsT=rows[0][:].bitcast(FP8X4), lhsT_scale=rows[1][:],
                rhs=words[:].bitcast(FP8X4), rhs_scale=scales, start=True, stop=True,
            )
            return bank

        def fma(name, x, scale, bias, dst=None, width=1, tag=None):
            res = dst if dst is not None else sb(name, width, tag=tag)[:]
            func = ACT.Copy if isinstance(bias, float) else ACT.Identity
            nc.scalar.activation(out=res, in_=x, func=func, scale=scale, bias=bias)
            return res

        def weighted(name, x, shift, op, weights, total, tag=None):
            res = sb(name, SLOTS, tag=tag)
            nc.vector.scalar_tensor_tensor(
                out=res[:], in0=x, scalar=shift, in1=weights, op0=op, op1=ALU.mult, accum_out=total
            )
            return res

        offsets = keep.tile([P, SLOTS // 16], U16, name="offsets")
        key_scales = sb("key_scales", TOKENS, U8)
        val_scales = sb("val_scales", TOKENS, U8)
        placed = sb("placed", TOKENS)
        ones = sb("ones", 1, tag="key_words")
        consts = sb("consts", 3)
        nc.vector.memset(ones[:], 1.0)
        nc.vector.memset(key_scales[:, : TOKENS // 2].bitcast(I32), 0)
        nc.gpsimd.memset(key_scales[:, TOKENS // 2 :].bitcast(I32), 0)
        nc.gpsimd.memset(val_scales[:].bitcast(I32), 0)
        nc.vector.tensor_scalar_mul(consts[:, 0:1], ones[:], 1.0 / ROOT)
        nc.vector.memset(consts[:, 1:2], ROOT)
        nc.vector.memset(consts[:, 2:3], -2.0)
        nc.vector.memset(placed[:, : TOKENS // 2 + 1], 0.0)
        nc.vector.memset(placed[:, TOKENS // 2 + 1 :], 0.0)

        nc.sync.dma_start(offsets[:], offs)
        query_raw = load_rows(sb("query_raw", PACK * ROWS), query)
        dquery_raw = load_rows(sb("dquery_raw", PACK * ROWS), dquery)
        load_scales(nc.sync, key_scales, keys_scales, 0)
        key_words = sb("key_words", TOKENS, U32)
        nc.sync.dma_start(out=key_words[:].bitcast(I32), in_=words_of(keys_words))
        load_scales(nc.gpsimd, val_scales, vals_scales, VALUE_PLANE)

        key_scales_g = gather("key_scales_g", key_scales, U8, "scales_g")
        query_bf = round_rows("query_bf", query_raw)
        gout_raw = load_rows(sb("gout_raw", PACK * ROWS, tag="query_raw"), gout)
        query_mx = quantise("query", query_bf, None)
        row_cols = sb("row_cols", 24, tag="query_bf")
        steep_col, th_col, sdot_col = row_cols[:, 0:1], row_cols[:, 8:9], row_cols[:, 16:17]
        nc.sync.dma_start(out=steep_col, in_=steep)
        nc.sync.dma_start(out=th_col, in_=th)
        nc.sync.dma_start(out=sdot_col, in_=sdot)
        val_words = sb("val_words", TOKENS, U32, tag="key_scales")
        nc.sync.dma_start(out=val_words[:].bitcast(I32), in_=words_of(vals_words))
        dquery_mx = quantise("dquery", round_rows("dquery_bf", dquery_raw), None)

        key_words_g = gather("key_words_g", key_words, U32, "words_g")
        a = product("a", query_mx, key_words_g, key_scales_g[:])
        t = product("t", dquery_mx, key_words_g, key_scales_g[:])
        gout_mx = quantise("gout", round_rows("gout_bf", gout_raw), "key_words")
        base_sb = sb("base_sb", TOKENS, tag="words_g")
        nc.sync.dma_start(out=base_sb[:], in_=base)

        neg_max = sb("neg_max", 1)
        nc.vector.tensor_reduce(out=neg_max[:], in_=a[:], axis=AX.X, op=ALU.max, negate=True)
        p = sb("p", SLOTS)
        z = sb("z", 1)
        nc.scalar.activation(out=p[:], in_=a[:], func=ACT.Exp, bias=neg_max[:], scale=1.0, accum_out=z[:])
        root = sb("root", 1)
        nc.gpsimd.tensor_tensor(out=root[:], in0=z[:], in1=consts[:, 0:1], op=ALU.pow)
        val_scales_g = gather("val_scales_g", val_scales, U8, "scales_g")
        by_sh = sb("by_sh", 2)
        inv_z = by_sh[:, 0:1]
        nc.vector.reciprocal(out=inv_z, in_=z[:])

        sums = sb("sums", 5)
        weighted("scrap_b", a[:], neg_max[:], ALU.add, p[:], sums[:, 0:1], "scrap_b")
        pt = weighted("pt", t[:], 1.0, ALU.mult, p[:], sums[:, 1:2])
        val_words_g = gather("val_words_g", val_words, U32, "scrap_b")
        c = product("c", gout_mx, val_words_g, val_scales_g[VALUE_PLANE:P, :])

        half_s = fma("half_s", steep_col, 0.5, 0.0)
        neg_half_s = fma("neg_half_s", steep_col, -0.5, 0.0)
        quarter_s = fma("quarter_s", steep_col, 0.25, 0.0)
        below_half_s = fma("below_half_s", steep_col, -0.5, -1.0)
        th_half_s = fma("th_half_s", th_col, half_s, quarter_s)
        fma("", sdot_col, -1.0, 0.0, dst=by_sh[:, 1:2])
        neg_inv_z = fma("neg_inv_z", inv_z, -1.0, 0.0)
        inv_z_256 = fma("inv_z_256", inv_z, 256.0, 0.0)
        back = sb("back", 1)
        nc.scalar.activation(out=back[:], in_=root[:], func=ACT.Exp, scale=-ROOT, bias=consts[:, 1:2])
        guess = fma("guess", root[:], ROOT, -ROOT)
        one_minus_b = fma("one_minus_b", sums[:, 0:1], neg_inv_z, 1.0)
        square = sb("square", 1, tag="square")
        nc.scalar.activation(out=square[:], in_=back[:], func=ACT.Square, scale=z[:], bias=consts[:, 2:3])
        gate_shift = fma("gate_shift", guess, neg_half_s, th_half_s)
        centre = fma("centre", neg_max[:], 1.0, one_minus_b)
        gate_bias = fma("gate_bias", one_minus_b, neg_half_s, gate_shift)
        neg_t = fma("neg_t", sums[:, 1:2], neg_inv_z, 0.0)
        tau = sb("tau", 1)
        nc.scalar.activation(out=tau[:], in_=square[:], func=ACT.Tanh, scale=quarter_s, bias=gate_bias)
        b = fma("b", a[:], 1.0, centre, width=SLOTS, tag="square")
        weighted("scrap_tb", b, 1.0, ALU.mult, pt[:], sums[:, 2:3], "key_scales")
        weighted("scrap_c", c[:], 1.0, ALU.mult, p[:], sums[:, 3:4])
        weighted("scrap_tc", c[:], 1.0, ALU.mult, pt[:], sums[:, 4:5])
        neg_t_over_z = fma("neg_t_over_z", neg_t, inv_z, 0.0)
        by_kappa = sb("by_kappa", 4)
        sh = fma("", tau[:], neg_half_s, half_s, dst=by_kappa[:, 0:1])
        kappa = fma("kappa", tau[:], inv_z_256, inv_z_256)
        fma("", tau[:], half_s, below_half_s, dst=by_kappa[:, 1:2])
        fma("", tau[:], neg_half_s, neg_half_s, dst=by_kappa[:, 2:3])
        fma("", tau[:], steep_col, -1.0, dst=by_kappa[:, 3:4])
        times_sh = fma("times_sh", by_sh[:], sh, 0.0, width=2)
        times_kappa = fma("times_kappa", by_kappa[:], kappa, 0.0, width=4)
        cov_tb = fma("cov_tb", sums[:, 2:3], inv_z, neg_t)
        shift = fma("shift", cov_tb, sh, neg_t)
        times_cov = fma("times_cov", times_kappa[:, 2:4], cov_tb, 0.0, width=2)
        halves = [slice(0, SLOTS // 2), slice(SLOTS // 2, SLOTS)]
        lam = fma("lam", sums[:, 3:4], times_sh[:, 0:1], times_sh[:, 1:2])
        neg_tc = fma("neg_tc", sums[:, 3:4], neg_t_over_z, 0.0)
        neg_c = fma("neg_c", sums[:, 3:4], neg_inv_z, 0.0)
        times_lam = fma("times_lam", times_cov, lam, 0.0, width=2)
        cov_tc = fma("cov_tc", sums[:, 4:5], inv_z, neg_tc)
        beta = fma("beta", cov_tc, times_kappa[:, 0:1], times_lam[:, 0:1])
        gamma = fma("gamma", cov_tc, times_kappa[:, 1:2], times_lam[:, 1:2])
        te = sb("te", SLOTS)
        for h in halves:
            fma("", t[:, h], 1.0, shift, dst=te[:, h])

        linear = sb("linear", SLOTS)
        inner = sb("inner", SLOTS)
        cross = sb("cross", SLOTS)
        bracket = sb("bracket", SLOTS)
        for h in halves:
            fma("", b[:, h], beta, gamma, dst=linear[:, h])
        for h in halves:
            nc.vector.scalar_tensor_tensor(out=inner[:, h], in0=b[:, h], scalar=lam, in1=c[:, h], op0=ALU.mult, op1=ALU.add)
        for h in halves:
            nc.vector.scalar_tensor_tensor(out=cross[:, h], in0=inner[:, h], scalar=neg_c, in1=te[:, h], op0=ALU.add, op1=ALU.mult)
        for h in halves:
            nc.vector.scalar_tensor_tensor(
                out=bracket[:, h], in0=cross[:, h], scalar=kappa, in1=linear[:, h], op0=ALU.mult, op1=ALU.add
            )
        nc.vector.tensor_tensor(out=placed[:].indirect(offsets[:]), in0=p[:], in1=bracket[:], op=ALU.mult)

        for i, width in enumerate(OUT_WIDTHS):
            c0 = sum(OUT_WIDTHS[:i])
            cols = slice(c0, c0 + width)
            result = sb("result_%d" % i, width)
            nc.vector.tensor_tensor(out=result[:], in0=base_sb[:, cols], in1=placed[:, cols], op=ALU.add)
            (nc.sync, nc.scalar)[i % 2].dma_start(out=out[:, cols], in_=result[:])
